import numpy as np
import ml_dtypes


def mxq(x, axis, fmt="e4m3"):
    dtype, down = {"e4m3": (ml_dtypes.float8_e4m3fn, 7), "e5m2": (ml_dtypes.float8_e5m2, 14)}[fmt]
    v = np.moveaxis(np.asarray(x, np.float32).astype(ml_dtypes.bfloat16).astype(np.float64), axis, -1)
    blocks = v.reshape(v.shape[:-1] + (-1, 32))
    amax = np.abs(blocks).max(-1, keepdims=True)
    byte = np.maximum(np.where(amax > 0, np.frexp(amax)[1] - 1 + 127, 0) - down, 1)
    scale = np.exp2(byte - 127.0)
    codes = (blocks / scale).astype(np.float32).astype(dtype).astype(np.float64)
    return np.moveaxis((codes * scale).reshape(v.shape), -1, axis)


WIDE = False


def mx_kscale(k):
    if not WIDE:
        return np.ones(k)
    levels = np.array([10, -10, 5, -5, 0])
    if k % 512:
        return np.exp2(np.random.permutation(np.resize(levels, k // 32))).repeat(32)
    a = np.empty((k // 512, 16))
    for p in range(k // 512):
        a[p, :8] = np.random.permutation(np.resize(levels, 8))
        for g in range(8):
            far = levels[np.abs(levels - a[p, g]) >= 10]
            a[p, g + 8] = far[np.random.randint(len(far))]
    return np.exp2(a.ravel()).repeat(32)


def f64(x):
    return np.asarray(x).astype(np.float64)


def striped(idx):
    return np.tile(idx.reshape(-1, 16).T, (8, 1)).astype(np.uint16)


def unstriped(offs):
    return offs[:16].T.reshape(-1).astype(np.int64)


def striped8(idx):
    return np.concatenate([x.reshape(-1, 16).T for x in idx]).astype(np.uint16)


def runs(offs, k):
    lists = np.stack([offs[16 * r : 16 * r + 16].T.reshape(-1) for r in range(8)]).astype(np.int64)
    return lists[np.arange(k) % 512 // 64]


def pack_weight(w):
    k, n = w.shape
    w = f64(np.asarray(w, np.float32).astype(ml_dtypes.bfloat16)).reshape(k // 32, 32, n)
    amax = np.abs(w).max(1)
    byte = np.clip(np.where(amax > 0, np.frexp(amax)[1] - 1 + 127 - 7, 1), 1, 254)
    scaled = (w * np.exp2(127.0 - byte)[:, None, :]).reshape(k, n).astype(np.float32)
    words = np.ascontiguousarray(scaled.reshape(k // 512, 128, 4, n).transpose(0, 1, 3, 2)).astype(ml_dtypes.float8_e4m3fn).view(np.uint8)
    return words, np.ascontiguousarray(byte.astype(np.uint8).reshape(k // 512, 16, n))


def unpack_weight(words, scales):
    g, p, n, _ = words.shape
    vals = np.ascontiguousarray(words).view(ml_dtypes.float8_e4m3fn).astype(np.float64) * np.repeat(np.exp2(scales.astype(np.float64) - 127.0), 8, axis=1)[..., None]
    return vals.transpose(0, 1, 3, 2).reshape(g * 512, n)


K, T, S, V, N, H = 512, 2048, 512, 256, 512, 512


def setup_inputs():
    n = np.random.standard_normal
    s = mx_kscale(K)[:, None]
    u = mx_kscale(H)
    packed_xT = pack_weight(n((K, T)) * s)
    perm = np.stack([np.random.permutation(S) for _ in range(8)])
    perm2 = np.stack([np.random.permutation(S) for _ in range(8)])
    return {
        "x_words": packed_xT[0],
        "x_scales": packed_xT[1],
        "w1": (n((K, H)) / np.sqrt(K) / s).astype(np.float32),
        "gn": (np.random.uniform(0.5, 1.5, (H, 1)) * u[:, None]).astype(np.float32),
        "w2": (n((H, N)) / np.sqrt(H) / u[:, None]).astype(np.float32),
        "offs": striped(np.random.permutation(T)[:S]),
        "la": striped8(perm[:, :V]),
        "lb": striped8(perm[:, V:]),
        "ma": striped8(perm2[:, :V]),
        "mb": striped8(perm2[:, V:]),
    }


def reference(x_words, x_scales, w1, gn, w2, offs, la, lb, ma, mb):
    xq = unpack_weight(x_words, x_scales)[:, unstriped(offs)]
    y = mxq(f64(w1), 0, "e4m3").T @ xq
    b = y[np.arange(H)[:, None], runs(lb, H)]
    a = y[np.arange(H)[:, None], runs(la, H)]
    c1 = 0.75 * ((a - b) / (np.abs(a - b) + 1))
    b1 = b + c1
    a1 = a - c1
    h0 = np.zeros((H, S))
    h0[np.arange(H)[:, None], runs(la, H)] = a1
    h = h0.copy()
    h[np.arange(H)[:, None], runs(lb, H)] = b1
    qv = h[np.arange(H)[:, None], runs(mb, H)]
    p = h[np.arange(H)[:, None], runs(ma, H)]
    c2 = 0.75 * ((p - qv) / (np.abs(p - qv) + 1))
    q1 = qv + c2
    p1 = p - c2
    h2 = np.zeros((H, S))
    h2[np.arange(H)[:, None], runs(ma, H)] = p1
    h3 = h2.copy()
    h3[np.arange(H)[:, None], runs(mb, H)] = q1
    z = f64(gn) * h3
    return mxq(f64(w2), 0, "e4m3").T @ mxq(z, 0, "e4m3")

@@ -1,0 +1,221 @@
+from contextlib import ExitStack
+
+import concourse.mybir as mybir
+
+F32 = mybir.dt.float32
+BF16 = mybir.dt.bfloat16
+I32 = mybir.dt.int32
+U32 = mybir.dt.uint32
+U16 = mybir.dt.uint16
+U8 = mybir.dt.uint8
+FP8X4 = mybir.dt.float8_e4m3fn_x4
+ACT = mybir.ActivationFunctionType
+ALU = mybir.AluOpType
+
+K, T, S, V, N, H = 512, 2048, 512, 256, 512, 512
+P = 128
+PACK = 4
+HALF = S // 2
+CHUNK = 128
+CHUNKS = S // CHUNK
+FLOPS = 2 * K * H * S + 2 * H * N * S
+
+
+def tile_picked_pbd2_none_p_kernel(
+    tc, x_words, x_scales, w1, gn, w2, offs, la, lb, ma, mb, out
+):
+    nc = tc.nc
+    with ExitStack() as ctx:
+        lists = ctx.enter_context(tc.tile_pool(name="lists", bufs=1))
+        keep = ctx.enter_context(tc.tile_pool(name="keep", bufs=1))
+        ring = ctx.enter_context(tc.tile_pool(name="ring", bufs=1))
+        psum = ctx.enter_context(tc.psum_pool(name="psum", bufs=1))
+
+        offs_sb = lists.tile([P, S // 16], U16, name="offs_sb")
+        pair_sb = {name: lists.tile([P, V // 16], U16, name=name + "_sb") for name in ("la", "lb", "ma", "mb")}
+
+        xw = keep.tile([P, T], U32, name="xw", align_bytes=64)
+        xs = keep.tile([P, T], U8, name="xs", align_bytes=64)
+        xs_rows = keep.tile([P, T], U8, name="xs_rows")
+        w1_raw = keep.tile([P, PACK, H], F32, name="w1_raw")
+        w2_raw = keep.tile([P, PACK, N], F32, name="w2_raw")
+
+        nc.vector.memset(xs[:].bitcast(I32), 0)
+        nc.sync.dma_start(offs_sb[:], offs)
+        for q in range(4):
+            nc.sync.dma_start(xs_rows[32 * q : 32 * q + 4, :].bitcast(I32), x_scales[0, 4 * q : 4 * q + 4, :].bitcast(I32))
+        nc.sync.dma_start(w1_raw[:], w1.rearrange("(p j) c -> p j c", j=PACK))
+        nc.sync.dma_start(xw[:].bitcast(I32), x_words[0].rearrange("p n t -> p (n t)").bitcast(I32))
+        nc.sync.dma_start(pair_sb["la"][:], la)
+        nc.sync.dma_start(pair_sb["lb"][:], lb)
+        nc.sync.dma_start(w2_raw[:], w2.rearrange("(p j) c -> p j c", j=PACK))
+        nc.sync.dma_start(pair_sb["ma"][:], ma)
+        nc.sync.dma_start(pair_sb["mb"][:], mb)
+
+        for q in range(4):
+            live = slice(32 * q, 32 * q + 4)
+            nc.vector.tensor_copy(out=xs[live, :].bitcast(I32), in_=xs_rows[live, :].bitcast(I32))
+        sg = keep.tile([P, S], U8, name="sg", align_bytes=64)
+        nc.vector.tensor_copy(out=sg[:], in_=xs[:].indirect(offs_sb[:]))
+
+        w1_b = keep.tile([P, H * PACK], BF16, name="w1_b", align_bytes=64)
+        nc.vector.tensor_copy(
+            out=w1_b[:].rearrange("p (t m j) -> p m t j", t=PACK, j=PACK),
+            in_=w1_raw[:].rearrange("p j (m t) -> p m t j", t=PACK),
+        )
+        w1_q = ring.tile([P, H], U32, name="w1_q", tag="rc-1", align_bytes=64)
+        w1_s = keep.tile([P, H], U8, name="w1_s", align_bytes=64)
+        nc.vector.quantize_mx(out=w1_q[:].bitcast(FP8X4), scales=w1_s[:], in_=w1_b[:])
+
+        xg = [keep.tile([P, HALF], U32, name=f"xg{h}", align_bytes=64) for h in range(2)]
+        for h in range(2):
+            nc.vector.tensor_copy(out=xg[h][:], in_=xw[:].indirect(offs_sb[:, 16 * h : 16 * (h + 1)]))
+
+        rows = [[keep.tile([P, S], F32, name=f"rows{s}_{t}") if s else None for t in range(PACK)] for s in range(3)]
+        banks = [psum.tile([P, HALF], F32, name=f"y_bank{i}", tag=f"bank{i}") for i in range(2 * PACK)]
+        for t in range(PACK):
+            cols = slice(P * t, P * (t + 1))
+            for h in range(2):
+                nc.tensor.matmul_mx(
+                    out=banks[2 * t + h][:], lhsT=w1_q[:, cols].bitcast(FP8X4), lhsT_scale=w1_s[:, cols],
+                    rhs=xg[h][:].bitcast(FP8X4), rhs_scale=sg[:, HALF * h : HALF * (h + 1)], start=True, stop=True,
+                )
+
+        def unload(t):
+            rows[0][t] = ring.tile([P, S], F32, name=f"rows0_{t}", tag=f"m{t - 2}", align_bytes=64)
+            nc.scalar.copy(out=rows[0][t][:, :HALF], in_=banks[2 * t][:])
+            if t == 0:
+                nc.vector.tensor_copy(out=rows[0][t][:, HALF:], in_=banks[2 * t + 1][:])
+            else:
+                nc.scalar.copy(out=rows[0][t][:, HALF:], in_=banks[2 * t + 1][:])
+
+        z_b = [keep.tile([P, CHUNK, PACK], BF16, name=f"z_b{c}", align_bytes=64) for c in range(CHUNKS)]
+
+        units = [(r, t) for r in range(2) for t in range(PACK)]
+        work = [{} for u in units]
+
+        def pair_lists(r):
+            return (pair_sb["la"], pair_sb["lb"]) if r == 0 else (pair_sb["ma"], pair_sb["mb"])
+
+        def fresh(u, name, tag):
+            work[u][name] = ring.tile([P, V], F32, name=f"{name}{u}", tag=tag, align_bytes=64)[:]
+            return work[u][name]
+
+        def pieces(u):
+            n = 2 if u < 1 else 1
+            return [(slice(V // n * i, V // n * (i + 1)), slice(V // 16 // n * i, V // 16 // n * (i + 1))) for i in range(n)]
+
+        def fetch(u):
+            r, t = units[u]
+            both = ring.tile([P, 2, V], F32, name=f"both{u}", tag=f"rc{u - 2}", align_bytes=64)
+            for side, name in enumerate("ab"):
+                work[u][name] = both[:, side, :]
+            for v, cols in pieces(u):
+                for side in range(2):
+                    picked = rows[r][t][:].indirect(pair_lists(r)[side][:, cols])
+                    if (u, side) == (0, 0):
+                        nc.vector.tensor_copy(out=both[:, side, v], in_=picked)
+                    else:
+                        nc.scalar.activation(out=both[:, side, v], in_=picked, func=ACT.Copy)
+
+        def diff(u, out):
+            work[u]["d"] = out
+            for v, cols in pieces(u):
+                nc.vector.tensor_tensor(out=out[:, v], in0=work[u]["a"][:, v], in1=work[u]["b"][:, v], op=ALU.subtract)
+
+        def factor(u):
+            w = work[u]
+            m, sq, rc, c = [fresh(u, name, f"{name}{u}") for name in ("m", "sq", "rc", "c")]
+            for v, cols in pieces(u):
+                nc.scalar.activation(out=m[:, v], in_=w["d"][:, v], func=ACT.Abs)
+            for v, cols in pieces(u):
+                nc.scalar.activation(out=sq[:, v], in_=m[:, v], func=ACT.Square, bias=1.0)
+            for v, cols in pieces(u):
+                nc.scalar.activation(out=rc[:, v], in_=sq[:, v], func=ACT.Abs_reciprocal_sqrt, scale=16.0 / 9.0)
+                nc.vector.tensor_tensor(out=c[:, v], in0=w["d"][:, v], in1=rc[:, v], op=ALU.mult)
+
+        def negate(u, out):
+            work[u]["nc"] = out
+            nc.scalar.activation(out=out, in_=work[u]["c"], func=ACT.Copy, scale=-1.0)
+
+        def put(u, side):
+            r, t = units[u]
+            w = work[u]
+            for v, cols in pieces(u) if side == 1 else pieces(len(units)):
+                nc.vector.tensor_tensor(
+                    out=rows[r + 1][t][:].indirect(pair_lists(r)[side][:, cols]),
+                    in0=w["ab"[side]][:, v], in1=w[("nc", "c")[side]][:, v], op=ALU.add,
+                )
+
+        def scale_z(gain, t, c):
+            nc.scalar.activation(
+                out=z_b[c][:, :, t], in_=rows[2][t][:, CHUNK * c : CHUNK * (c + 1)], func=ACT.Copy, scale=gain[:, t : t + 1]
+            )
+
+        w2_q = keep.tile([P, N], U32, name="w2_q", align_bytes=64)
+        w2_s = keep.tile([P, N], U8, name="w2_s", align_bytes=64)
+
+        def prepare_w2(i):
+            cols = slice(P * i, P * (i + 1))
+            w2_b = keep.tile([P, P, PACK], BF16, name=f"w2_b{i}", align_bytes=64)
+            nc.vector.tensor_copy(out=w2_b[:], in_=w2_raw[:, :, cols].rearrange("p j c -> p c j"))
+            nc.vector.quantize_mx(out=w2_q[:, cols].bitcast(FP8X4), scales=w2_s[:, cols], in_=w2_b[:].rearrange("p c j -> p (c j)"))
+
+        last = len(units) - 1
+        unload(0)
+        fetch(0)
+        diff(0, fresh(0, "d", "d0"))
+        unload(1)
+        fetch(1)
+        diff(1, fresh(1, "d", "d1"))
+        gain = None
+        for u in range(len(units)):
+            factor(u)
+            after = ring.tile([P, 2, V], F32, name=f"after{u}", tag=f"sq{u}", align_bytes=64)
+            if u == 0:
+                pass
+            if 1 <= u < last:
+                diff(u + 1, after[:, 0, :])
+            if u == 6:
+                gain = ring.tile([P, PACK], F32, name="gain", tag=f"m{u}", align_bytes=64)
+                nc.sync.dma_start(gain[:], gn.rearrange("(p t) o -> p (t o)", t=PACK))
+            if u >= 1:
+                negate(u - 1, after[:, 1, :])
+                put(u - 1, 0)
+            put(u, 1)
+            if u < 1 - 1:
+                negate(u, fresh(u, "nc", f"nc{u}"))
+                put(u, 0)
+            if u + 2 < PACK:
+                unload(u + 2)
+            if u + 2 <= last:
+                fetch(u + 2)
+        for c in range(CHUNKS):
+            scale_z(gain, 0, c)
+        negate(last, fresh(last, "nc", "nc_last"))
+        put(last, 0)
+        for t in (1, 2):
+            for c in range(CHUNKS):
+                scale_z(gain, t, c)
+        for i in range(PACK):
+            prepare_w2(i)
+
+        out_v = out.rearrange("(i p) j -> p i j", p=P)
+        for c in range(CHUNKS):
+            scale_z(gain, PACK - 1, c)
+            z_q = keep.tile([P, CHUNK], U32, name=f"z_q{c}", align_bytes=64)
+            z_s = keep.tile([P, CHUNK], U8, name=f"z_s{c}", align_bytes=64)
+            nc.vector.quantize_mx(out=z_q[:].bitcast(FP8X4), scales=z_s[:], in_=z_b[c][:].rearrange("p s j -> p (s j)"))
+            bank = psum.tile([P, PACK, CHUNK], F32, name=f"o_bank{c}", tag=f"bank{c}")
+            for i in range(PACK):
+                cols = slice(P * i, P * (i + 1))
+                nc.tensor.matmul_mx(
+                    out=bank[:, i, :], lhsT=w2_q[:, cols].bitcast(FP8X4), lhsT_scale=w2_s[:, cols],
+                    rhs=z_q[:].bitcast(FP8X4), rhs_scale=z_s[:], start=True, stop=True,
+                )
+            res = keep.tile([P, PACK, CHUNK], F32, name=f"res{c}")
+            if c < 2:
+                nc.vector.tensor_copy(out=res[:], in_=bank[:])
+            else:
+                nc.scalar.copy(out=res[:], in_=bank[:])
+            nc.sync.dma_start(out_v[:, :, CHUNK * c : CHUNK * (c + 1)], res[:])

@@ -16,7 +16,7 @@ K, T, S, V, N, H = 512, 2048, 512, 256, 512, 512
 P = 128
 PACK = 4
 HALF = S // 2
-CHUNK = 128
+CHUNK = 256
 CHUNKS = S // CHUNK
 FLOPS = 2 * K * H * S + 2 * H * N * S
 
@@ -41,6 +41,9 @@ def tile_picked_pbd2_none_p_kernel(
         w2_raw = keep.tile([P, PACK, N], F32, name="w2_raw")
 
         nc.vector.memset(xs[:].bitcast(I32), 0)
+        warm = keep.tile([P, 2], F32, name="warm")
+        nc.vector.memset(warm[:, 0:1], 1.0)
+        nc.scalar.activation(out=warm[:, 1:2], in_=warm[:, 0:1], func=ACT.Abs_reciprocal_sqrt)
         nc.sync.dma_start(offs_sb[:], offs)
         for q in range(4):
             nc.sync.dma_start(xs_rows[32 * q : 32 * q + 4, :].bitcast(I32), x_scales[0, 4 * q : 4 * q + 4, :].bitcast(I32))
@@ -71,7 +74,7 @@ def tile_picked_pbd2_none_p_kernel(
         for h in range(2):
             nc.vector.tensor_copy(out=xg[h][:], in_=xw[:].indirect(offs_sb[:, 16 * h : 16 * (h + 1)]))
 
-        rows = [[keep.tile([P, S], F32, name=f"rows{s}_{t}") if s else None for t in range(PACK)] for s in range(3)]
+        rows = [[None] * PACK for s in range(3)]
         banks = [psum.tile([P, HALF], F32, name=f"y_bank{i}", tag=f"bank{i}") for i in range(2 * PACK)]
         for t in range(PACK):
             cols = slice(P * t, P * (t + 1))
@@ -141,6 +144,8 @@ def tile_picked_pbd2_none_p_kernel(
         def put(u, side):
             r, t = units[u]
             w = work[u]
+            if side == 1:
+                rows[r + 1][t] = ring.tile([P, S], F32, name=f"rows{r + 1}_{t}", tag=f"c{u - 1}" if u == len(units) - 1 else f"rows{u}", align_bytes=64)
             for v, cols in pieces(u) if side == 1 else pieces(len(units)):
                 nc.vector.tensor_tensor(
                     out=rows[r + 1][t][:].indirect(pair_lists(r)[side][:, cols]),
@@ -148,9 +153,11 @@ def tile_picked_pbd2_none_p_kernel(
                 )
 
         def scale_z(gain, t, c):
-            nc.scalar.activation(
-                out=z_b[c][:, :, t], in_=rows[2][t][:, CHUNK * c : CHUNK * (c + 1)], func=ACT.Copy, scale=gain[:, t : t + 1]
-            )
+            src = rows[2][t][:, CHUNK * c : CHUNK * (c + 1)]
+            if t >= 2 and c == 0:
+                nc.vector.tensor_scalar(out=z_b[c][:, :, t], in0=src, scalar1=gain[:, t : t + 1], scalar2=None, op0=ALU.mult)
+            else:
+                nc.scalar.activation(out=z_b[c][:, :, t], in_=src, func=ACT.Copy, scale=gain[:, t : t + 1])
 
         w2_q = keep.tile([P, N], U32, name="w2_q", align_bytes=64)
         w2_s = keep.tile([P, N], U8, name="w2_s", align_bytes=64)
@@ -176,7 +183,7 @@ def tile_picked_pbd2_none_p_kernel(
                 pass
             if 1 <= u < last:
                 diff(u + 1, after[:, 0, :])
-            if u == 6:
+            if u == 7:
                 gain = ring.tile([P, PACK], F32, name="gain", tag=f"m{u}", align_bytes=64)
                 nc.sync.dma_start(gain[:], gn.rearrange("(p t) o -> p (t o)", t=PACK))
             if u >= 1:
@@ -194,7 +201,7 @@ def tile_picked_pbd2_none_p_kernel(
             scale_z(gain, 0, c)
         negate(last, fresh(last, "nc", "nc_last"))
         put(last, 0)
-        for t in (1, 2):
+        for t in (1, 2, 3):
             for c in range(CHUNKS):
                 scale_z(gain, t, c)
         for i in range(PACK):
@@ -202,20 +209,21 @@ def tile_picked_pbd2_none_p_kernel(
 
         out_v = out.rearrange("(i p) j -> p i j", p=P)
         for c in range(CHUNKS):
-            scale_z(gain, PACK - 1, c)
             z_q = keep.tile([P, CHUNK], U32, name=f"z_q{c}", align_bytes=64)
             z_s = keep.tile([P, CHUNK], U8, name=f"z_s{c}", align_bytes=64)
             nc.vector.quantize_mx(out=z_q[:].bitcast(FP8X4), scales=z_s[:], in_=z_b[c][:].rearrange("p s j -> p (s j)"))
-            bank = psum.tile([P, PACK, CHUNK], F32, name=f"o_bank{c}", tag=f"bank{c}")
-            for i in range(PACK):
-                cols = slice(P * i, P * (i + 1))
-                nc.tensor.matmul_mx(
-                    out=bank[:, i, :], lhsT=w2_q[:, cols].bitcast(FP8X4), lhsT_scale=w2_s[:, cols],
-                    rhs=z_q[:].bitcast(FP8X4), rhs_scale=z_s[:], start=True, stop=True,
-                )
-            res = keep.tile([P, PACK, CHUNK], F32, name=f"res{c}")
-            if c < 2:
-                nc.vector.tensor_copy(out=res[:], in_=bank[:])
-            else:
-                nc.scalar.copy(out=res[:], in_=bank[:])
-            nc.sync.dma_start(out_v[:, :, CHUNK * c : CHUNK * (c + 1)], res[:])
+            for k in range(PACK // 1):
+                n = PACK // 1 * c + k
+                bank = psum.tile([P, 1, CHUNK], F32, name=f"o_bank{n}", tag=f"bank{n}")
+                for i in range(1):
+                    cols = slice(P * (1 * k + i), P * (1 * k + i + 1))
+                    nc.tensor.matmul_mx(
+                        out=bank[:, i, :], lhsT=w2_q[:, cols].bitcast(FP8X4), lhsT_scale=w2_s[:, cols],
+                        rhs=z_q[:].bitcast(FP8X4), rhs_scale=z_s[:], start=True, stop=True,
+                    )
+                res = keep.tile([P, 1, CHUNK], F32, name=f"res{n}")
+                if n in (4, 5, 7):
+                    nc.vector.tensor_copy(out=res[:], in_=bank[:])
+                else:
+                    nc.scalar.copy(out=res[:], in_=bank[:])
+                nc.sync.dma_start(out_v[:, 1 * k : 1 * (k + 1), CHUNK * c : CHUNK * (c + 1)], res[:])

from contextlib import ExitStack

import concourse.mybir as mybir

F32 = mybir.dt.float32
BF16 = mybir.dt.bfloat16
I32 = mybir.dt.int32
U32 = mybir.dt.uint32
U16 = mybir.dt.uint16
U8 = mybir.dt.uint8
FP8X4 = mybir.dt.float8_e4m3fn_x4
ACT = mybir.ActivationFunctionType
ALU = mybir.AluOpType

K, T, S, V, N, H = 512, 2048, 512, 256, 512, 512
P = 128
PACK = 4
HALF = S // 2
CHUNK = 256
CHUNKS = S // CHUNK
FLOPS = 2 * K * H * S + 2 * H * N * S


def tile_picked_pbd2_none_p_kernel(
    tc, x_words, x_scales, w1, gn, w2, offs, la, lb, ma, mb, out
):
    nc = tc.nc
    with ExitStack() as ctx:
        lists = ctx.enter_context(tc.tile_pool(name="lists", bufs=1))
        keep = ctx.enter_context(tc.tile_pool(name="keep", bufs=1))
        ring = ctx.enter_context(tc.tile_pool(name="ring", bufs=1))
        psum = ctx.enter_context(tc.psum_pool(name="psum", bufs=1))

        offs_sb = lists.tile([P, S // 16], U16, name="offs_sb")
        pair_sb = {name: lists.tile([P, V // 16], U16, name=name + "_sb") for name in ("la", "lb", "ma", "mb")}

        xw = keep.tile([P, T], U32, name="xw", align_bytes=64)
        xs = keep.tile([P, T], U8, name="xs", align_bytes=64)
        xs_rows = keep.tile([P, T], U8, name="xs_rows")
        w1_raw = keep.tile([P, PACK, H], F32, name="w1_raw")
        w2_raw = keep.tile([P, PACK, N], F32, name="w2_raw")

        nc.vector.memset(xs[:].bitcast(I32), 0)
        warm = keep.tile([P, 2], F32, name="warm")
        nc.vector.memset(warm[:, 0:1], 1.0)
        nc.scalar.activation(out=warm[:, 1:2], in_=warm[:, 0:1], func=ACT.Abs_reciprocal_sqrt)
        nc.sync.dma_start(offs_sb[:], offs)
        for q in range(4):
            nc.sync.dma_start(xs_rows[32 * q : 32 * q + 4, :].bitcast(I32), x_scales[0, 4 * q : 4 * q + 4, :].bitcast(I32))
        nc.sync.dma_start(w1_raw[:], w1.rearrange("(p j) c -> p j c", j=PACK))
        nc.sync.dma_start(xw[:].bitcast(I32), x_words[0].rearrange("p n t -> p (n t)").bitcast(I32))
        nc.sync.dma_start(pair_sb["la"][:], la)
        nc.sync.dma_start(pair_sb["lb"][:], lb)
        nc.sync.dma_start(w2_raw[:], w2.rearrange("(p j) c -> p j c", j=PACK))
        nc.sync.dma_start(pair_sb["ma"][:], ma)
        nc.sync.dma_start(pair_sb["mb"][:], mb)

        for q in range(4):
            live = slice(32 * q, 32 * q + 4)
            nc.vector.tensor_copy(out=xs[live, :].bitcast(I32), in_=xs_rows[live, :].bitcast(I32))
        sg = keep.tile([P, S], U8, name="sg", align_bytes=64)
        nc.vector.tensor_copy(out=sg[:], in_=xs[:].indirect(offs_sb[:]))

        w1_b = keep.tile([P, H * PACK], BF16, name="w1_b", align_bytes=64)
        nc.vector.tensor_copy(
            out=w1_b[:].rearrange("p (t m j) -> p m t j", t=PACK, j=PACK),
            in_=w1_raw[:].rearrange("p j (m t) -> p m t j", t=PACK),
        )
        w1_q = ring.tile([P, H], U32, name="w1_q", tag="rc-1", align_bytes=64)
        w1_s = keep.tile([P, H], U8, name="w1_s", align_bytes=64)
        nc.vector.quantize_mx(out=w1_q[:].bitcast(FP8X4), scales=w1_s[:], in_=w1_b[:])

        xg = [keep.tile([P, HALF], U32, name=f"xg{h}", align_bytes=64) for h in range(2)]
        for h in range(2):
            nc.vector.tensor_copy(out=xg[h][:], in_=xw[:].indirect(offs_sb[:, 16 * h : 16 * (h + 1)]))

        rows = [[None] * PACK for s in range(3)]
        banks = [psum.tile([P, HALF], F32, name=f"y_bank{i}", tag=f"bank{i}") for i in range(2 * PACK)]
        for t in range(PACK):
            cols = slice(P * t, P * (t + 1))
            for h in range(2):
                nc.tensor.matmul_mx(
                    out=banks[2 * t + h][:], lhsT=w1_q[:, cols].bitcast(FP8X4), lhsT_scale=w1_s[:, cols],
                    rhs=xg[h][:].bitcast(FP8X4), rhs_scale=sg[:, HALF * h : HALF * (h + 1)], start=True, stop=True,
                )

        def unload(t):
            rows[0][t] = ring.tile([P, S], F32, name=f"rows0_{t}", tag=f"m{t - 2}", align_bytes=64)
            nc.scalar.copy(out=rows[0][t][:, :HALF], in_=banks[2 * t][:])
            if t == 0:
                nc.vector.tensor_copy(out=rows[0][t][:, HALF:], in_=banks[2 * t + 1][:])
            else:
                nc.scalar.copy(out=rows[0][t][:, HALF:], in_=banks[2 * t + 1][:])

        z_b = [keep.tile([P, CHUNK, PACK], BF16, name=f"z_b{c}", align_bytes=64) for c in range(CHUNKS)]

        units = [(r, t) for r in range(2) for t in range(PACK)]
        work = [{} for u in units]

        def pair_lists(r):
            return (pair_sb["la"], pair_sb["lb"]) if r == 0 else (pair_sb["ma"], pair_sb["mb"])

        def fresh(u, name, tag):
            work[u][name] = ring.tile([P, V], F32, name=f"{name}{u}", tag=tag, align_bytes=64)[:]
            return work[u][name]

        def pieces(u):
            n = 2 if u < 1 else 1
            return [(slice(V // n * i, V // n * (i + 1)), slice(V // 16 // n * i, V // 16 // n * (i + 1))) for i in range(n)]

        def fetch(u):
            r, t = units[u]
            both = ring.tile([P, 2, V], F32, name=f"both{u}", tag=f"rc{u - 2}", align_bytes=64)
            for side, name in enumerate("ab"):
                work[u][name] = both[:, side, :]
            for v, cols in pieces(u):
                for side in range(2):
                    picked = rows[r][t][:].indirect(pair_lists(r)[side][:, cols])
                    if (u, side) == (0, 0):
                        nc.vector.tensor_copy(out=both[:, side, v], in_=picked)
                    else:
                        nc.scalar.activation(out=both[:, side, v], in_=picked, func=ACT.Copy)

        def diff(u, out):
            work[u]["d"] = out
            for v, cols in pieces(u):
                nc.vector.tensor_tensor(out=out[:, v], in0=work[u]["a"][:, v], in1=work[u]["b"][:, v], op=ALU.subtract)

        def factor(u):
            w = work[u]
            m, sq, rc, c = [fresh(u, name, f"{name}{u}") for name in ("m", "sq", "rc", "c")]
            for v, cols in pieces(u):
                nc.scalar.activation(out=m[:, v], in_=w["d"][:, v], func=ACT.Abs)
            for v, cols in pieces(u):
                nc.scalar.activation(out=sq[:, v], in_=m[:, v], func=ACT.Square, bias=1.0)
            for v, cols in pieces(u):
                nc.scalar.activation(out=rc[:, v], in_=sq[:, v], func=ACT.Abs_reciprocal_sqrt, scale=16.0 / 9.0)
                nc.vector.tensor_tensor(out=c[:, v], in0=w["d"][:, v], in1=rc[:, v], op=ALU.mult)

        def negate(u, out):
            work[u]["nc"] = out
            nc.scalar.activation(out=out, in_=work[u]["c"], func=ACT.Copy, scale=-1.0)

        def put(u, side):
            r, t = units[u]
            w = work[u]
            if side == 1:
                rows[r + 1][t] = ring.tile([P, S], F32, name=f"rows{r + 1}_{t}", tag=f"c{u - 1}" if u == len(units) - 1 else f"rows{u}", align_bytes=64)
            for v, cols in pieces(u) if side == 1 else pieces(len(units)):
                nc.vector.tensor_tensor(
                    out=rows[r + 1][t][:].indirect(pair_lists(r)[side][:, cols]),
                    in0=w["ab"[side]][:, v], in1=w[("nc", "c")[side]][:, v], op=ALU.add,
                )

        def scale_z(gain, t, c):
            src = rows[2][t][:, CHUNK * c : CHUNK * (c + 1)]
            if t >= 2 and c == 0:
                nc.vector.tensor_scalar(out=z_b[c][:, :, t], in0=src, scalar1=gain[:, t : t + 1], scalar2=None, op0=ALU.mult)
            else:
                nc.scalar.activation(out=z_b[c][:, :, t], in_=src, func=ACT.Copy, scale=gain[:, t : t + 1])

        w2_q = keep.tile([P, N], U32, name="w2_q", align_bytes=64)
        w2_s = keep.tile([P, N], U8, name="w2_s", align_bytes=64)

        def prepare_w2(i):
            cols = slice(P * i, P * (i + 1))
            w2_b = keep.tile([P, P, PACK], BF16, name=f"w2_b{i}", align_bytes=64)
            nc.vector.tensor_copy(out=w2_b[:], in_=w2_raw[:, :, cols].rearrange("p j c -> p c j"))
            nc.vector.quantize_mx(out=w2_q[:, cols].bitcast(FP8X4), scales=w2_s[:, cols], in_=w2_b[:].rearrange("p c j -> p (c j)"))

        last = len(units) - 1
        unload(0)
        fetch(0)
        diff(0, fresh(0, "d", "d0"))
        unload(1)
        fetch(1)
        diff(1, fresh(1, "d", "d1"))
        gain = None
        for u in range(len(units)):
            factor(u)
            after = ring.tile([P, 2, V], F32, name=f"after{u}", tag=f"sq{u}", align_bytes=64)
            if u == 0:
                pass
            if 1 <= u < last:
                diff(u + 1, after[:, 0, :])
            if u == 7:
                gain = ring.tile([P, PACK], F32, name="gain", tag=f"m{u}", align_bytes=64)
                nc.sync.dma_start(gain[:], gn.rearrange("(p t) o -> p (t o)", t=PACK))
            if u >= 1:
                negate(u - 1, after[:, 1, :])
                put(u - 1, 0)
            put(u, 1)
            if u < 1 - 1:
                negate(u, fresh(u, "nc", f"nc{u}"))
                put(u, 0)
            if u + 2 < PACK:
                unload(u + 2)
            if u + 2 <= last:
                fetch(u + 2)
        for c in range(CHUNKS):
            scale_z(gain, 0, c)
        negate(last, fresh(last, "nc", "nc_last"))
        put(last, 0)
        for t in (1, 2, 3):
            for c in range(CHUNKS):
                scale_z(gain, t, c)
        for i in range(PACK):
            prepare_w2(i)

        out_v = out.rearrange("(i p) j -> p i j", p=P)
        for c in range(CHUNKS):
            z_q = keep.tile([P, CHUNK], U32, name=f"z_q{c}", align_bytes=64)
            z_s = keep.tile([P, CHUNK], U8, name=f"z_s{c}", align_bytes=64)
            nc.vector.quantize_mx(out=z_q[:].bitcast(FP8X4), scales=z_s[:], in_=z_b[c][:].rearrange("p s j -> p (s j)"))
            for k in range(PACK // 1):
                n = PACK // 1 * c + k
                bank = psum.tile([P, 1, CHUNK], F32, name=f"o_bank{n}", tag=f"bank{n}")
                for i in range(1):
                    cols = slice(P * (1 * k + i), P * (1 * k + i + 1))
                    nc.tensor.matmul_mx(
                        out=bank[:, i, :], lhsT=w2_q[:, cols].bitcast(FP8X4), lhsT_scale=w2_s[:, cols],
                        rhs=z_q[:].bitcast(FP8X4), rhs_scale=z_s[:], start=True, stop=True,
                    )
                res = keep.tile([P, 1, CHUNK], F32, name=f"res{n}")
                if n in (4, 5, 7):
                    nc.vector.tensor_copy(out=res[:], in_=bank[:])
                else:
                    nc.scalar.copy(out=res[:], in_=bank[:])
                nc.sync.dma_start(out_v[:, 1 * k : 1 * (k + 1), CHUNK * c : CHUNK * (c + 1)], res[:])
